import numpy as np, ml_dtypes
CORES = [34,162,290,418,42,426]
N = 6
W, KW, DIL = 256, 3, 2
H = (KW // 2) * DIL
def setup_inputs(rng):
    return {"x": rng.standard_normal((N, 128, W), dtype=np.float32).astype(ml_dtypes.bfloat16), "w": rng.standard_normal((N, 128, KW * 128), dtype=np.float32).astype(ml_dtypes.bfloat16)}
def setup_inputs_big(rng):
    d = setup_inputs(rng)
    for k in ("x", "w"): d[k] = (d[k].astype(np.float32) * 1024.0).astype(d[k].dtype)
    return d
def setup_inputs_small(rng):
    d = setup_inputs(rng)
    for k in ("x", "w"): d[k] = (d[k].astype(np.float32) * (1 / 1024.0)).astype(d[k].dtype)
    return d
def reference(x, w):
    X, W_ = x.astype(np.float64), w.astype(np.float64)
    g = np.concatenate(list(X), axis=1)
    p = np.pad(g, ((0, 0), (H, H)))
    y = np.zeros((N, 128, W))
    for r in range(N):
        for i in range(KW):
            y[r] += W_[r][:, 128 * i:128 * i + 128].T @ p[:, W * r + i * DIL:W * r + i * DIL + W]
    return {"y": y.astype(ml_dtypes.bfloat16 if x.dtype != np.float64 else np.float64)}

@@ -1,0 +1,80 @@
+from concourse.bass import DstId, RemoteDMATransfer
+
+P = 128
+NP = 128
+ENG = 4
+
+SCRATCH = {
+    "xs": ("sbuf", [P, NP, 2], "bfloat16"),
+    "ws": ("sbuf", [P, 3 * P], "bfloat16"),
+    "halo": ("sbuf", [P, 2, 2], "bfloat16"),
+    "ys": ("sbuf", [P, NP, 2], "bfloat16"),
+    "pin": ("psum", [P, 256, 2], "float32"),
+    "ped": ("psum", [P, 256, 2], "float32"),
+}
+SEMAPHORES = ["xin", "win", "sent", "got", "mm_in", "mm_ed", "rounded", "stored"]
+
+
+def _engines(mask, n, skip):
+    bits = [b for b in range(mask.bit_length()) if (mask >> b) & 1]
+    m = 0
+    for b in bits[skip:skip + n]:
+        m |= 1 << b
+    return m
+
+
+def rank_program(g, core, T, topo):
+    rank = T.rank_of(core)
+    if rank is None:
+        return
+    n = len(T.cores)
+    left = T.cores[rank - 1] if rank > 0 else None
+    right = T.cores[rank + 1] if rank < n - 1 else None
+    S = T.sem
+    xs, ws, halo, ys, pin, ped = T.xs, T.ws, T.halo, T.ys, T.pin, T.ped
+    w0, w1, w2 = ws[:, 0:P], ws[:, P:2 * P], ws[:, 2 * P:3 * P]
+
+    g.sync.dma_start(xs[:], T.x[:, :]).then_inc(S.xin, 16)
+    g.sync.dma_start(ws[:], T.w[:, :]).then_inc(S.win, 16)
+
+    g.wait_ge(S.xin, 16)
+    transfers = []
+    for dst, src_ap, dst_ap in ((left, xs[:, 0, :], halo[:, 1, :]), (right, xs[:, NP - 1, :], halo[:, 0, :])):
+        if dst is None:
+            continue
+        rid, pid = topo.addr(dst, core)
+        transfers.append(RemoteDMATransfer(
+            dst_ids=[DstId(rid=rid, pnc=pid)],
+            dma_engine_mask=_engines(topo.mask(core, dst), ENG, ENG * len(transfers)),
+            remote_sem=S.got, src=src_ap, dst=dst_ap))
+    g.remote_dma_fused(transfers, local_sem=S.sent)
+    g.wait_ge(S.sent, ENG * len(transfers))
+
+    te = g.tensor
+    te.wait_ge(S.xin, 16)
+    te.wait_ge(S.win, 16)
+    te.matmul(pin[:, 1:NP - 1, :], w1, xs[:, 1:NP - 1, :], start=True, stop=False)
+    te.matmul(pin[:, 1:NP - 1, :], w0, xs[:, 0:NP - 2, :], start=False, stop=False)
+    te.matmul(pin[:, 1:NP - 1, :], w2, xs[:, 2:NP, :], start=False, stop=True).then_inc(S.mm_in, 1)
+    te.matmul(ped[:, 0:2, :], w1, xs[:, 0:NP:NP - 1, :], start=True, stop=False)
+    te.matmul(ped[:, 0, :], w2, xs[:, 1, :], start=False, stop=False)
+    te.matmul(ped[:, 1, :], w0, xs[:, NP - 2, :], start=False, stop=False)
+    te.wait_ge(S.got, ENG * len(transfers))
+    late = []
+    if left is not None:
+        late.append((ped[:, 0, :], w0, halo[:, 0, :]))
+    if right is not None:
+        late.append((ped[:, 1, :], w2, halo[:, 1, :]))
+    for i, (o, wt, h) in enumerate(late):
+        mm = te.matmul(o, wt, h, start=False, stop=(i == len(late) - 1))
+    mm.then_inc(S.mm_ed, 1)
+
+    ve = g.vector
+    ve.wait_ge(S.mm_in, 1)
+    ve.tensor_copy(ys[:, 1:NP - 1, :], pin[:, 1:NP - 1, :]).then_inc(S.rounded, 1)
+    ve.wait_ge(S.mm_ed, 1)
+    ve.tensor_copy(ys[:, 0:NP:NP - 1, :], ped[:, 0:2, :]).then_inc(S.rounded, 1)
+
+    g.sync.wait_ge(S.rounded, 2)
+    g.sync.dma_start(T.y[:, :], ys[:]).then_inc(S.stored, 16)
+    g.sync.wait_ge(S.stored, 16)

@@ -1,54 +1,82 @@
-from concourse.bass import DstId, RemoteDMATransfer
-
 P = 128
 NP = 128
-ENG = 4
 
 SCRATCH = {
+    "xe": ("sbuf", [P, 2, 2], "bfloat16"),
     "xs": ("sbuf", [P, NP, 2], "bfloat16"),
     "ws": ("sbuf", [P, 3 * P], "bfloat16"),
-    "halo": ("sbuf", [P, 2, 2], "bfloat16"),
+    "hl": ("sbuf", [P, 2], "bfloat16"),
+    "hr": ("sbuf", [P, 2], "bfloat16"),
     "ys": ("sbuf", [P, NP, 2], "bfloat16"),
+    "yl": ("sbuf", [P, 2], "bfloat16"),
+    "yr": ("sbuf", [P, 2], "bfloat16"),
     "pin": ("psum", [P, 256, 2], "float32"),
-    "ped": ("psum", [P, 256, 2], "float32"),
+    "pl": ("psum", [P, 512], "float32"),
+    "pr": ("psum", [P, 512], "float32"),
 }
-SEMAPHORES = ["xin", "win", "sent", "got", "mm_in", "mm_ed", "rounded", "stored"]
+SEMAPHORES = ["xe0", "xe1", "xin", "win", "sent", "got0", "got1", "mm_in", "mm0", "mm1", "r_in", "r0", "r1",
+              "st_in", "st0", "st1"]
 
 
-def _engines(mask, n, skip):
+def _links(topo, a, b):
+    if topo.rack(topo.host(a)) != topo.rack(topo.host(b)):
+        return 1 if topo.chip(a) == topo.chip(b) else 2
+    return 1 if (topo.same_plane(a, b) or topo.mates(a, b)) else 2
+
+
+def _half(mask, k):
     bits = [b for b in range(mask.bit_length()) if (mask >> b) & 1]
+    h = len(bits) // 2
     m = 0
-    for b in bits[skip:skip + n]:
+    for b in bits[k * h:(k + 1) * h]:
         m |= 1 << b
     return m
+
+
+def _order(topo, cores, r):
+    sides = [s for s in (0, 1) if 0 <= r + 2 * s - 1 < len(cores)]
+    sides.sort(key=lambda s: -_links(topo, cores[r], cores[r + 2 * s - 1]))
+    return sides
 
 
 def rank_program(g, core, T, topo):
     rank = T.rank_of(core)
     if rank is None:
         return
-    n = len(T.cores)
-    left = T.cores[rank - 1] if rank > 0 else None
-    right = T.cores[rank + 1] if rank < n - 1 else None
+    cores = T.cores
     S = T.sem
-    xs, ws, halo, ys, pin, ped = T.xs, T.ws, T.halo, T.ys, T.pin, T.ped
+    xe, xs, ws, ys, pin = T.xe, T.xs, T.ws, T.ys, T.pin
     w0, w1, w2 = ws[:, 0:P], ws[:, P:2 * P], ws[:, 2 * P:3 * P]
+    W = 2 * NP
+    q = (g.sync, g.scalar)
+    halo = (T.hl, T.hr)
+    yo = (T.yl, T.yr)
+    ps = (T.pl, T.pr)
+    xcols = (T.x[:, 0:2], T.x[:, W - 2:W])
+    ycols = (T.y[:, 0:2], T.y[:, W - 2:W])
+    serve = _order(topo, cores, rank)
 
+    for k, s in enumerate(serve):
+        q[k].dma_start(xe[:, s, :], xcols[s]).then_inc(S["xe%d" % s], 16)
     g.sync.dma_start(xs[:], T.x[:, :]).then_inc(S.xin, 16)
-    g.sync.dma_start(ws[:], T.w[:, :]).then_inc(S.win, 16)
+    g.scalar.dma_start(ws[:], T.w[:, :]).then_inc(S.win, 16)
 
-    g.wait_ge(S.xin, 16)
-    transfers = []
-    for dst, src_ap, dst_ap in ((left, xs[:, 0, :], halo[:, 1, :]), (right, xs[:, NP - 1, :], halo[:, 0, :])):
-        if dst is None:
-            continue
+    out = 0
+    for k, s in enumerate(serve):
+        dst = cores[rank + 2 * s - 1]
         rid, pid = topo.addr(dst, core)
-        transfers.append(RemoteDMATransfer(
-            dst_ids=[DstId(rid=rid, pnc=pid)],
-            dma_engine_mask=_engines(topo.mask(core, dst), ENG, ENG * len(transfers)),
-            remote_sem=S.got, src=src_ap, dst=dst_ap))
-    g.remote_dma_fused(transfers, local_sem=S.sent)
-    g.wait_ge(S.sent, ENG * len(transfers))
+        m = _half(topo.mask(core, dst), k)
+        g.wait_ge(S["xe%d" % s], 16)
+        g.remote_dma(halo[1 - s][:, :], xe[:, s, :], S["got%d" % (1 - s)], S.sent, pid, rid, m)
+        out += bin(m).count("1")
+    g.wait_ge(S.sent, out)
+
+    arrive = []
+    for s in serve:
+        nb = rank + 2 * s - 1
+        k = _order(topo, cores, nb).index(1 - s)
+        arrive.append((k, s, bin(_half(topo.mask(cores[nb], core), k)).count("1")))
+    arrive.sort()
 
     te = g.tensor
     te.wait_ge(S.xin, 16)
@@ -56,25 +84,30 @@ def rank_program(g, core, T, topo):
     te.matmul(pin[:, 1:NP - 1, :], w1, xs[:, 1:NP - 1, :], start=True, stop=False)
     te.matmul(pin[:, 1:NP - 1, :], w0, xs[:, 0:NP - 2, :], start=False, stop=False)
     te.matmul(pin[:, 1:NP - 1, :], w2, xs[:, 2:NP, :], start=False, stop=True).then_inc(S.mm_in, 1)
-    te.matmul(ped[:, 0:2, :], w1, xs[:, 0:NP:NP - 1, :], start=True, stop=False)
-    te.matmul(ped[:, 0, :], w2, xs[:, 1, :], start=False, stop=False)
-    te.matmul(ped[:, 1, :], w0, xs[:, NP - 2, :], start=False, stop=False)
-    te.wait_ge(S.got, ENG * len(transfers))
-    late = []
-    if left is not None:
-        late.append((ped[:, 0, :], w0, halo[:, 0, :]))
-    if right is not None:
-        late.append((ped[:, 1, :], w2, halo[:, 1, :]))
-    for i, (o, wt, h) in enumerate(late):
-        mm = te.matmul(o, wt, h, start=False, stop=(i == len(late) - 1))
-    mm.then_inc(S.mm_ed, 1)
+    own = ((0, 1, w2), (NP - 1, NP - 2, w0))
+    for s in (0, 1):
+        e, i, wt = own[s]
+        te.matmul(ps[s][:, 0:2], w1, xs[:, e, :], start=True, stop=False)
+        mm = te.matmul(ps[s][:, 0:2], wt, xs[:, i, :], start=False, stop=(s not in serve))
+        if s not in serve:
+            mm.then_inc(S["mm%d" % s], 1)
+    for k, s, cnt in arrive:
+        te.wait_ge(S["got%d" % s], cnt)
+        te.matmul(ps[s][:, 0:2], (w0, w2)[s], halo[s][:, :], start=False, stop=True).then_inc(S["mm%d" % s], 1)
 
+    closing = [s for s in (0, 1) if s not in serve] + [s for k, s, cnt in arrive]
     ve = g.vector
     ve.wait_ge(S.mm_in, 1)
-    ve.tensor_copy(ys[:, 1:NP - 1, :], pin[:, 1:NP - 1, :]).then_inc(S.rounded, 1)
-    ve.wait_ge(S.mm_ed, 1)
-    ve.tensor_copy(ys[:, 0:NP:NP - 1, :], ped[:, 0:2, :]).then_inc(S.rounded, 1)
+    ve.tensor_copy(ys[:, 1:NP - 1, :], pin[:, 1:NP - 1, :]).then_inc(S.r_in, 1)
+    for s in closing:
+        ve.wait_ge(S["mm%d" % s], 1)
+        ve.tensor_copy(yo[s][:, :], ps[s][:, 0:2]).then_inc(S["r%d" % s], 1)
 
-    g.sync.wait_ge(S.rounded, 2)
-    g.sync.dma_start(T.y[:, :], ys[:]).then_inc(S.stored, 16)
-    g.sync.wait_ge(S.stored, 16)
+    g.sync.wait_ge(S.r_in, 1)
+    g.sync.dma_start(T.y[:, 2:W - 2], ys[:, 1:NP - 1, :]).then_inc(S.st_in, 16)
+    for s in (0, 1):
+        q[s].wait_ge(S["r%d" % s], 1)
+        q[s].dma_start(ycols[s], yo[s][:, :]).then_inc(S["st%d" % s], 16)
+    g.sync.wait_ge(S.st_in, 16)
+    for s in (0, 1):
+        q[s].wait_ge(S["st%d" % s], 16)

P = 128
NP = 128

SCRATCH = {
    "xe": ("sbuf", [P, 2, 2], "bfloat16"),
    "xs": ("sbuf", [P, NP, 2], "bfloat16"),
    "ws": ("sbuf", [P, 3 * P], "bfloat16"),
    "hl": ("sbuf", [P, 2], "bfloat16"),
    "hr": ("sbuf", [P, 2], "bfloat16"),
    "ys": ("sbuf", [P, NP, 2], "bfloat16"),
    "yl": ("sbuf", [P, 2], "bfloat16"),
    "yr": ("sbuf", [P, 2], "bfloat16"),
    "pin": ("psum", [P, 256, 2], "float32"),
    "pl": ("psum", [P, 512], "float32"),
    "pr": ("psum", [P, 512], "float32"),
}
SEMAPHORES = ["xe0", "xe1", "xin", "win", "sent", "got0", "got1", "mm_in", "mm0", "mm1", "r_in", "r0", "r1",
              "st_in", "st0", "st1"]


def _links(topo, a, b):
    if topo.rack(topo.host(a)) != topo.rack(topo.host(b)):
        return 1 if topo.chip(a) == topo.chip(b) else 2
    return 1 if (topo.same_plane(a, b) or topo.mates(a, b)) else 2


def _half(mask, k):
    bits = [b for b in range(mask.bit_length()) if (mask >> b) & 1]
    h = len(bits) // 2
    m = 0
    for b in bits[k * h:(k + 1) * h]:
        m |= 1 << b
    return m


def _order(topo, cores, r):
    sides = [s for s in (0, 1) if 0 <= r + 2 * s - 1 < len(cores)]
    sides.sort(key=lambda s: -_links(topo, cores[r], cores[r + 2 * s - 1]))
    return sides


def rank_program(g, core, T, topo):
    rank = T.rank_of(core)
    if rank is None:
        return
    cores = T.cores
    S = T.sem
    xe, xs, ws, ys, pin = T.xe, T.xs, T.ws, T.ys, T.pin
    w0, w1, w2 = ws[:, 0:P], ws[:, P:2 * P], ws[:, 2 * P:3 * P]
    W = 2 * NP
    q = (g.sync, g.scalar)
    halo = (T.hl, T.hr)
    yo = (T.yl, T.yr)
    ps = (T.pl, T.pr)
    xcols = (T.x[:, 0:2], T.x[:, W - 2:W])
    ycols = (T.y[:, 0:2], T.y[:, W - 2:W])
    serve = _order(topo, cores, rank)

    for k, s in enumerate(serve):
        q[k].dma_start(xe[:, s, :], xcols[s]).then_inc(S["xe%d" % s], 16)
    g.sync.dma_start(xs[:], T.x[:, :]).then_inc(S.xin, 16)
    g.scalar.dma_start(ws[:], T.w[:, :]).then_inc(S.win, 16)

    out = 0
    for k, s in enumerate(serve):
        dst = cores[rank + 2 * s - 1]
        rid, pid = topo.addr(dst, core)
        m = _half(topo.mask(core, dst), k)
        g.wait_ge(S["xe%d" % s], 16)
        g.remote_dma(halo[1 - s][:, :], xe[:, s, :], S["got%d" % (1 - s)], S.sent, pid, rid, m)
        out += bin(m).count("1")
    g.wait_ge(S.sent, out)

    arrive = []
    for s in serve:
        nb = rank + 2 * s - 1
        k = _order(topo, cores, nb).index(1 - s)
        arrive.append((k, s, bin(_half(topo.mask(cores[nb], core), k)).count("1")))
    arrive.sort()

    te = g.tensor
    te.wait_ge(S.xin, 16)
    te.wait_ge(S.win, 16)
    te.matmul(pin[:, 1:NP - 1, :], w1, xs[:, 1:NP - 1, :], start=True, stop=False)
    te.matmul(pin[:, 1:NP - 1, :], w0, xs[:, 0:NP - 2, :], start=False, stop=False)
    te.matmul(pin[:, 1:NP - 1, :], w2, xs[:, 2:NP, :], start=False, stop=True).then_inc(S.mm_in, 1)
    own = ((0, 1, w2), (NP - 1, NP - 2, w0))
    for s in (0, 1):
        e, i, wt = own[s]
        te.matmul(ps[s][:, 0:2], w1, xs[:, e, :], start=True, stop=False)
        mm = te.matmul(ps[s][:, 0:2], wt, xs[:, i, :], start=False, stop=(s not in serve))
        if s not in serve:
            mm.then_inc(S["mm%d" % s], 1)
    for k, s, cnt in arrive:
        te.wait_ge(S["got%d" % s], cnt)
        te.matmul(ps[s][:, 0:2], (w0, w2)[s], halo[s][:, :], start=False, stop=True).then_inc(S["mm%d" % s], 1)

    closing = [s for s in (0, 1) if s not in serve] + [s for k, s, cnt in arrive]
    ve = g.vector
    ve.wait_ge(S.mm_in, 1)
    ve.tensor_copy(ys[:, 1:NP - 1, :], pin[:, 1:NP - 1, :]).then_inc(S.r_in, 1)
    for s in closing:
        ve.wait_ge(S["mm%d" % s], 1)
        ve.tensor_copy(yo[s][:, :], ps[s][:, 0:2]).then_inc(S["r%d" % s], 1)

    g.sync.wait_ge(S.r_in, 1)
    g.sync.dma_start(T.y[:, 2:W - 2], ys[:, 1:NP - 1, :]).then_inc(S.st_in, 16)
    for s in (0, 1):
        q[s].wait_ge(S["r%d" % s], 1)
        q[s].dma_start(ycols[s], yo[s][:, :]).then_inc(S["st%d" % s], 16)
    g.sync.wait_ge(S.st_in, 16)
    for s in (0, 1):
        q[s].wait_ge(S["st%d" % s], 16)
